import numpy as np, ml_dtypes
CORES = [1,3,5,9,11,13]
N = 6
NP, NBK, TK, CAP = 3, 6, 32, 8
DEST = [[5,3,3,3,3,4],[5,5,3,4,4,3],[5,3,4,5,3,5]]
def setup_inputs(rng):
    return {"x": rng.standard_normal((N, 128, NBK * TK), dtype=np.float32).astype(ml_dtypes.bfloat16), "w": (rng.standard_normal((N, 128, 128), dtype=np.float32) / 8).astype(ml_dtypes.bfloat16)}
def setup_inputs_big(rng):
    d = setup_inputs(rng)
    for k in ("x", "w"): d[k] = (d[k].astype(np.float32) * 1024.0).astype(d[k].dtype)
    return d
def setup_inputs_small(rng):
    d = setup_inputs(rng)
    for k in ("x", "w"): d[k] = (d[k].astype(np.float32) * (1 / 1024.0)).astype(d[k].dtype)
    return d
def setup_inputs_apart(rng):
    d = setup_inputs(rng)
    f = (10.0 ** rng.permutation(np.linspace(-1.5, 1.5, N))).astype(np.float32).reshape(N, 1, 1)
    for k in ("x", "w"): d[k] = (d[k].astype(np.float32) * f).astype(d[k].dtype)
    return d
def reference(x, w):
    X, W = x.astype(np.float64), w.astype(np.float64)
    y = np.full((N, 128, CAP * TK), np.nan); n = [0] * N
    for p in range(NP):
        for c in range(NBK):
            q = DEST[p][c]
            y[q][:, TK * n[q]:TK * n[q] + TK] = W[q].T @ np.maximum(W[p].T @ X[p][:, TK * c:TK * c + TK], 0.0)
            n[q] += 1
    return {"y": y.astype(ml_dtypes.bfloat16 if x.dtype != np.float64 else np.float64)}

@@ -1,0 +1,191 @@
+from concourse.bass import DstId, RemoteDMATransfer
+from concourse.mybir import AluOpType
+
+SIM_CORES = 16
+NPR, NBK, TK, CAP = 3, 6, 32, 8
+HW = NBK * TK
+
+ON_CHIP_ENGINES = 16
+OFF_CHIP_ENGINES = 8
+
+SCRATCH = {
+    "xs": ("sbuf", [128, HW], "bfloat16"),
+    "ws": ("sbuf", [128, 128], "bfloat16"),
+    "zs": ("sbuf", [128, HW], "float32"),
+    "hp": ("psum", [128, 512], "float32"),
+    "hs": ("sbuf", [128, HW], "bfloat16"),
+    "land": ("sbuf", [128, NPR * HW], "bfloat16"),
+    "hq": ("sbuf", [128, NPR * HW], "bfloat16"),
+    "yp0": ("psum", [128, 512], "float32"),
+    "yp1": ("psum", [128, 512], "float32"),
+    "yp2": ("psum", [128, 512], "float32"),
+    "ys": ("sbuf", [128, CAP * TK], "bfloat16"),
+}
+SEMAPHORES = ["ldx", "ldw", "zf", "mm", "act", "sent",
+              "rin0", "rin1", "rin2", "arr0", "arr1", "arr2",
+              "ym0", "ym1", "ym2", "yc0", "yc1", "yc2", "st0", "st1", "st2"]
+
+
+def _shares(total, k):
+    each = 1
+    while each * 2 * k <= total:
+        each *= 2
+    sizes = [each] * k
+    for i in range(k):
+        if sum(sizes) + sizes[i] <= total:
+            sizes[i] *= 2
+    return sizes
+
+
+def _call(topo, src, transfers):
+    m = None
+    away = False
+    for tr in transfers:
+        for d in tr[3]:
+            k = topo.mask(src, d[0])
+            m = k if m is None else m & k
+            away = away or topo.chip(d[0]) != topo.chip(src)
+    engs = [b for b in range(m.bit_length()) if (m >> b) & 1]
+    engs = engs[:OFF_CHIP_ENGINES if away else ON_CHIP_ENGINES]
+    out = []
+    at = 0
+    for tr, n in zip(transfers, _shares(len(engs), len(transfers))):
+        out.append((tr, engs[at:at + n]))
+        at += n
+    return out
+
+
+def _plan(T, topo):
+    dest = T.tables["DEST"]
+    cores = T.cores
+    qs = sorted({q for row in dest for q in row})
+    fill = {q: 0 for q in qs}
+    grp = {}
+    for p in range(len(dest)):
+        for c, q in enumerate(dest[p]):
+            if (p, q) not in grp:
+                grp[(p, q)] = [fill[q], []]
+            grp[(p, q)][1].append(c)
+            fill[q] += 1
+    runs, calls, fwd, arrive, direct = {}, {}, {}, {}, {}
+    for p in range(len(dest)):
+        src = cores[p]
+        mine = sorted([q for q in qs if (p, q) in grp], key=lambda q: (len(grp[(p, q)][1]), q))
+        off, wid, order = {}, {}, []
+        for q in mine:
+            off[q], wid[q] = len(order), len(grp[(p, q)][1])
+            order += grp[(p, q)][1]
+        rs = []
+        for s, c in enumerate(order):
+            if rs and rs[-1][0] + rs[-1][2] == c:
+                rs[-1][2] += 1
+            else:
+                rs.append([c, s, 1])
+        runs[p] = rs
+
+        def to_q(buf, base, q, w):
+            return (buf, base + off[q] * TK, w * TK, [(cores[q], "hq", p * HW)], "arr%d" % p)
+
+        def note(call):
+            for tr, engs in call:
+                arrive[(p, tr[3][0][0])] = len(engs)
+            return call
+
+        direct[p] = all(topo.may_write(src, cores[q]) for q in mine)
+        calls[p] = []
+        if direct[p]:
+            for w in sorted({wid[q] for q in mine}):
+                calls[p].append(note(_call(topo, src, [to_q("hs", 0, q, w) for q in mine[::-1] if wid[q] == w])))
+            continue
+        ports = [c for c in range(SIM_CORES)
+                 if c != src and topo.chip(c) == topo.chip(src) and topo.die(c) == topo.die(src)
+                 and all(topo.may_write(c, cores[q]) for q in mine)]
+        ports.sort(key=lambda c: (T.rank_of(c) is None, c))
+        rest, wide = mine[:-1], mine[-1]
+        base = p * HW
+        sem = "rin%d" % p
+        if not rest:
+            shares = [(ports[-1], off[wide], wid[wide])]
+        else:
+            shares = [(ports[0], 0, off[wide]), (ports[-1], off[wide], wid[wide])]
+        if len({s[2] for s in shares}) == 1:
+            call = _call(topo, src, [("hs", s[1] * TK, s[2] * TK, [(s[0], "land", base + s[1] * TK)], sem)
+                                     for s in shares])
+            got = [len(e) for tr, e in call]
+        else:
+            call = _call(topo, src, [("hs", 0, HW, [(s[0], "land", base) for s in shares], sem)])
+            got = [len(call[0][1])] * len(shares)
+        calls[p].append(call)
+        if rest:
+            w = max(wid[q] for q in rest)
+            fwd.setdefault(ports[0], []).append(
+                (sem, got[0], note(_call(topo, ports[0], [to_q("land", base, q, w) for q in rest[::-1]]))))
+        fwd.setdefault(ports[-1], []).append(
+            (sem, got[-1], note(_call(topo, ports[-1], [to_q("land", base, wide, wid[wide])]))))
+    return grp, runs, calls, fwd, arrive, direct
+
+
+def _emit(g, T, topo, call):
+    trs = []
+    n = 0
+    for tr, engs in call:
+        mask = 0
+        for b in engs:
+            mask |= 1 << b
+        n += len(engs)
+        ids = [topo.addr(d[0]) for d in tr[3]]
+        src = T[tr[0]][:, tr[1]:tr[1] + tr[2]]
+        dsts = [T[d[1]][:, d[2]:d[2] + tr[2]] for d in tr[3]]
+        if len(call) == 1 and len(dsts) == 1:
+            g.remote_dma(dsts[0], src, T.sem[tr[4]], T.sem.sent, ids[0][1], ids[0][0], mask)
+            return n
+        trs.append(RemoteDMATransfer(dst_ids=[DstId(rid=a[0], pnc=a[1]) for a in ids], dma_engine_mask=mask,
+                                     remote_sem=T.sem[tr[4]], srcs=[src], dsts=dsts))
+    g.remote_dma_fused(trs, local_sem=T.sem.sent)
+    return n
+
+
+def rank_program(g, core, T, topo):
+    grp, runs, calls, fwd, arrive, direct = _plan(T, topo)
+    rank = T.rank_of(core)
+    S = T.sem
+    sent = 0
+
+    if rank in runs:
+        g.sync.dma_start(T.xs[:], T.x[:]).then_inc(S.ldx, 16)
+        g.scalar.dma_start(T.ws[:], T.w[:]).then_inc(S.ldw, 16)
+        g.vector.memset(T.zs[:], 0.0).then_inc(S.zf, 1)
+        g.tensor.wait_ge(S.ldw, 16)
+        g.tensor.wait_ge(S.ldx, 16)
+        for c, s, k in runs[rank]:
+            g.tensor.matmul(T.hp[:, s * TK:(s + k) * TK], T.ws[:], T.xs[:, c * TK:(c + k) * TK], True, True).then_inc(S.mm, 1)
+        g.vector.wait_ge(S.zf, 1)
+        g.vector.wait_ge(S.mm, len(runs[rank]))
+        g.vector.tensor_tensor(T.hs[:], T.hp[:, 0:HW], T.zs[:], AluOpType.max).then_inc(S.act, 1)
+        g.wait_ge(S.act, 1)
+        for call in calls[rank]:
+            sent += _emit(g, T, topo, call)
+
+    for sem, n, call in fwd.get(core, []):
+        g.wait_ge(S[sem], n)
+        sent += _emit(g, T, topo, call)
+    if sent:
+        g.wait_ge(S.sent, sent)
+
+    senders = [p for p in sorted(runs, key=lambda p: (not direct[p], p)) if (p, rank) in grp]
+    if senders:
+        g.sync.dma_start(T.ws[:], T.w[:]).then_inc(S.ldw, 16)
+        g.tensor.wait_ge(S.ldw, 16)
+        for i, p in enumerate(senders):
+            slot, blocks = grp[(p, rank)]
+            a, w = slot * TK, len(blocks) * TK
+            ps = T["yp%d" % p]
+            g.tensor.wait_ge(S["arr%d" % p], arrive[(p, core)])
+            g.tensor.matmul(ps[:, 0:w], T.ws[:], T.hq[:, p * HW:p * HW + w], True, True).then_inc(S["ym%d" % p], 1)
+            g.vector.wait_ge(S["ym%d" % p], 1)
+            g.vector.tensor_copy(T.ys[:, a:a + w], ps[:, 0:w]).then_inc(S["yc%d" % p], 1)
+            dq = g.scalar if i % 2 else g.sync
+            dq.wait_ge(S["yc%d" % p], 1)
+            dq.dma_start(T.y[:, a:a + w], T.ys[:, a:a + w]).then_inc(S["st%d" % p], 16)
+        for p in senders:
+            g.wait_ge(S["st%d" % p], 16)

@@ -4,55 +4,34 @@ from concourse.mybir import AluOpType
 SIM_CORES = 16
 NPR, NBK, TK, CAP = 3, 6, 32, 8
 HW = NBK * TK
-
-ON_CHIP_ENGINES = 16
-OFF_CHIP_ENGINES = 8
+HAND = 8
 
 SCRATCH = {
     "xs": ("sbuf", [128, HW], "bfloat16"),
     "ws": ("sbuf", [128, 128], "bfloat16"),
     "zs": ("sbuf", [128, HW], "float32"),
-    "hp": ("psum", [128, 512], "float32"),
+    "hp0": ("psum", [128, 512], "float32"),
+    "hp1": ("psum", [128, 512], "float32"),
     "hs": ("sbuf", [128, HW], "bfloat16"),
-    "land": ("sbuf", [128, NPR * HW], "bfloat16"),
-    "hq": ("sbuf", [128, NPR * HW], "bfloat16"),
+    "land": ("sbuf", [128, 2 * HW], "bfloat16"),
+    "hq": ("sbuf", [128, 4 * HW], "bfloat16"),
     "yp0": ("psum", [128, 512], "float32"),
     "yp1": ("psum", [128, 512], "float32"),
     "yp2": ("psum", [128, 512], "float32"),
     "ys": ("sbuf", [128, CAP * TK], "bfloat16"),
 }
-SEMAPHORES = ["ldx", "ldw", "zf", "mm", "act", "sent",
-              "rin0", "rin1", "rin2", "arr0", "arr1", "arr2",
-              "ym0", "ym1", "ym2", "yc0", "yc1", "yc2", "st0", "st1", "st2"]
+SEMAPHORES = ["ldx", "ldw", "zf", "mm0", "mm1", "act0", "act1", "sent",
+              "rin00", "rin01", "rin10", "rin11", "arr0", "arr1", "arr2", "ym0", "ym1", "ym2", "yc", "st"]
 
 
-def _shares(total, k):
-    each = 1
-    while each * 2 * k <= total:
-        each *= 2
-    sizes = [each] * k
-    for i in range(k):
-        if sum(sizes) + sizes[i] <= total:
-            sizes[i] *= 2
-    return sizes
-
-
-def _call(topo, src, transfers):
-    m = None
-    away = False
-    for tr in transfers:
-        for d in tr[3]:
-            k = topo.mask(src, d[0])
-            m = k if m is None else m & k
-            away = away or topo.chip(d[0]) != topo.chip(src)
-    engs = [b for b in range(m.bit_length()) if (m >> b) & 1]
-    engs = engs[:OFF_CHIP_ENGINES if away else ON_CHIP_ENGINES]
-    out = []
-    at = 0
-    for tr, n in zip(transfers, _shares(len(engs), len(transfers))):
-        out.append((tr, engs[at:at + n]))
-        at += n
-    return out
+def _runs(order, a, b):
+    rs = []
+    for s in range(a, b):
+        if rs and rs[-1][0] + rs[-1][2] == order[s]:
+            rs[-1][2] += 1
+        else:
+            rs.append([order[s], s, 1])
+    return rs
 
 
 def _plan(T, topo):
@@ -67,125 +46,149 @@ def _plan(T, topo):
                 grp[(p, q)] = [fill[q], []]
             grp[(p, q)][1].append(c)
             fill[q] += 1
-    runs, calls, fwd, arrive, direct = {}, {}, {}, {}, {}
-    for p in range(len(dest)):
-        src = cores[p]
-        mine = sorted([q for q in qs if (p, q) in grp], key=lambda q: (len(grp[(p, q)][1]), q))
-        off, wid, order = {}, {}, []
-        for q in mine:
-            off[q], wid[q] = len(order), len(grp[(p, q)][1])
-            order += grp[(p, q)][1]
-        rs = []
-        for s, c in enumerate(order):
-            if rs and rs[-1][0] + rs[-1][2] == c:
-                rs[-1][2] += 1
-            else:
-                rs.append([c, s, 1])
-        runs[p] = rs
+    wid = {k: len(v[1]) for k, v in grp.items()}
 
-        def to_q(buf, base, q, w):
-            return (buf, base + off[q] * TK, w * TK, [(cores[q], "hq", p * HW)], "arr%d" % p)
+    def engines(src, dst, most=None):
+        m = topo.mask(src, dst)
+        e = [b for b in range(m.bit_length()) if (m >> b) & 1]
+        return e if most is None else e[::len(e) // most]
 
-        def note(call):
-            for tr, engs in call:
-                arrive[(p, tr[3][0][0])] = len(engs)
-            return call
+    def idle_port(p):
+        return [c for c in range(SIM_CORES)
+                if T.rank_of(c) is None and topo.chip(c) == topo.chip(cores[p]) and topo.die(c) == topo.die(cores[p])
+                and all(topo.may_write(c, cores[q]) for q in qs)][0]
 
-        direct[p] = all(topo.may_write(src, cores[q]) for q in mine)
-        calls[p] = []
-        if direct[p]:
-            for w in sorted({wid[q] for q in mine}):
-                calls[p].append(note(_call(topo, src, [to_q("hs", 0, q, w) for q in mine[::-1] if wid[q] == w])))
-            continue
-        ports = [c for c in range(SIM_CORES)
-                 if c != src and topo.chip(c) == topo.chip(src) and topo.die(c) == topo.die(src)
-                 and all(topo.may_write(c, cores[q]) for q in mine)]
-        ports.sort(key=lambda c: (T.rank_of(c) is None, c))
-        rest, wide = mine[:-1], mine[-1]
-        base = p * HW
-        sem = "rin%d" % p
-        if not rest:
-            shares = [(ports[-1], off[wide], wid[wide])]
-        else:
-            shares = [(ports[0], 0, off[wide]), (ports[-1], off[wide], wid[wide])]
-        if len({s[2] for s in shares}) == 1:
-            call = _call(topo, src, [("hs", s[1] * TK, s[2] * TK, [(s[0], "land", base + s[1] * TK)], sem)
-                                     for s in shares])
-            got = [len(e) for tr, e in call]
-        else:
-            call = _call(topo, src, [("hs", 0, HW, [(s[0], "land", base) for s in shares], sem)])
-            got = [len(call[0][1])] * len(shares)
-        calls[p].append(call)
-        if rest:
-            w = max(wid[q] for q in rest)
-            fwd.setdefault(ports[0], []).append(
-                (sem, got[0], note(_call(topo, ports[0], [to_q("land", base, q, w) for q in rest[::-1]]))))
-        fwd.setdefault(ports[-1], []).append(
-            (sem, got[-1], note(_call(topo, ports[-1], [to_q("land", base, wide, wid[wide])]))))
-    return grp, runs, calls, fwd, arrive, direct
+    own = [p for p in range(len(dest)) if all(topo.may_write(cores[p], cores[q]) for q in qs)]
+    hp = own[0]
+    hub = cores[hp]
+    p1, p2 = [p for p in range(len(dest)) if p != hp]
+    qa, qb, qc = qs
+    stages = {}
+    got = {q: [] for q in qs}
+    fwd = {}
+
+    order = [c for q in qs for c in grp[(hp, q)][1]]
+    cl, at = [], 0
+    for q in qs:
+        e = engines(hub, cores[q])
+        cl.append([("hs", at * TK, wid[(hp, q)] * TK, cores[q], "hq", 0, "arr0", e)])
+        got[q].append(("arr0", len(e), 0, [(hp, wid[(hp, q)])]))
+        at += wid[(hp, q)]
+    stages[hp] = [(_runs(order, 0, len(order)), 0, len(order), cl)]
+
+    at = 0
+    where = {}
+    for k, (p, lone, rest) in enumerate(((p2, qc, [qa, qb]), (p1, qa, [qb, qc]))):
+        order = grp[(p, lone)][1] + [c for q in rest for c in grp[(p, q)][1]]
+        via = idle_port(p)
+        n0, n1 = wid[(p, lone)], sum(wid[(p, q)] for q in rest)
+        e = engines(cores[p], via, HAND)
+        e2 = engines(via, cores[lone])
+        stages[p] = [(_runs(order, 0, n0), 0, n0, [[("hs", 0, n0 * TK, via, "land", 0, "rin%d0" % k, e)]])]
+        fwd[via] = [([("rin%d0" % k, len(e))], [("land", 0, n0 * TK, cores[lone], "hq", 3 * HW, "arr2", e2)])]
+        got[lone].append(("arr2", len(e2), 3 * HW, [(p, n0)]))
+        e = engines(cores[p], hub, HAND)
+        stages[p].append((_runs(order, n0, n0 + n1), n0, n1,
+                          [[("hs", n0 * TK, n1 * TK, hub, "land", at * TK, "rin%d1" % k, e)]]))
+        where[p] = ("rin%d1" % k, len(e))
+        at += n1
+    joint = []
+    at = 0
+    for q, ps in ((qa, [p2]), (qb, [p2, p1]), (qc, [p1])):
+        joint.append((q, at, [(p, wid[(p, q)]) for p in ps]))
+        at += sum(wid[(p, q)] for p in ps)
+    calls = {}
+    for j in joint:
+        calls.setdefault(sum(k for p, k in j[2]), []).append(j)
+    fwd[hub] = []
+    for n in sorted(calls, key=lambda n: (len(calls[n]), n)):
+        js = calls[n]
+        parts = [js] if len(js) in (1, 2, 4, 8) else [[j] for j in js]
+        for js in parts:
+            need, call = [], []
+            for i, (q, a, ps) in enumerate(js):
+                e = engines(hub, cores[q])
+                m = len(e) // len(js)
+                e = e[i * m:(i + 1) * m]
+                call.append(("land", a * TK, n * TK, cores[q], "hq", HW, "arr1", e))
+                need += [where[p] for p, k in ps if where[p] not in need]
+                arr = ("arr1", len(e), HW, ps)
+                if fwd[hub]:
+                    got[q].append(arr)
+                else:
+                    got[q].insert(1, arr)
+            fwd[hub].append((need, call))
+    return grp, stages, fwd, got, fill
 
 
 def _emit(g, T, topo, call):
     trs = []
     n = 0
-    for tr, engs in call:
+    for w in call:
         mask = 0
-        for b in engs:
+        for b in w[7]:
             mask |= 1 << b
-        n += len(engs)
-        ids = [topo.addr(d[0]) for d in tr[3]]
-        src = T[tr[0]][:, tr[1]:tr[1] + tr[2]]
-        dsts = [T[d[1]][:, d[2]:d[2] + tr[2]] for d in tr[3]]
-        if len(call) == 1 and len(dsts) == 1:
-            g.remote_dma(dsts[0], src, T.sem[tr[4]], T.sem.sent, ids[0][1], ids[0][0], mask)
+        n += len(w[7])
+        a = topo.addr(w[3])
+        src, dst = T[w[0]][:, w[1]:w[1] + w[2]], T[w[4]][:, w[5]:w[5] + w[2]]
+        if len(call) == 1:
+            g.remote_dma(dst, src, T.sem[w[6]], T.sem.sent, a[1], a[0], mask)
             return n
-        trs.append(RemoteDMATransfer(dst_ids=[DstId(rid=a[0], pnc=a[1]) for a in ids], dma_engine_mask=mask,
-                                     remote_sem=T.sem[tr[4]], srcs=[src], dsts=dsts))
+        trs.append(RemoteDMATransfer(dst_ids=[DstId(rid=a[0], pnc=a[1])], dma_engine_mask=mask,
+                                     remote_sem=T.sem[w[6]], srcs=[src], dsts=[dst]))
     g.remote_dma_fused(trs, local_sem=T.sem.sent)
     return n
 
 
 def rank_program(g, core, T, topo):
-    grp, runs, calls, fwd, arrive, direct = _plan(T, topo)
+    grp, stages, fwd, got, fill = _plan(T, topo)
     rank = T.rank_of(core)
     S = T.sem
     sent = 0
 
-    if rank in runs:
+    if rank in stages:
         g.sync.dma_start(T.xs[:], T.x[:]).then_inc(S.ldx, 16)
         g.scalar.dma_start(T.ws[:], T.w[:]).then_inc(S.ldw, 16)
         g.vector.memset(T.zs[:], 0.0).then_inc(S.zf, 1)
         g.tensor.wait_ge(S.ldw, 16)
         g.tensor.wait_ge(S.ldx, 16)
-        for c, s, k in runs[rank]:
-            g.tensor.matmul(T.hp[:, s * TK:(s + k) * TK], T.ws[:], T.xs[:, c * TK:(c + k) * TK], True, True).then_inc(S.mm, 1)
         g.vector.wait_ge(S.zf, 1)
-        g.vector.wait_ge(S.mm, len(runs[rank]))
-        g.vector.tensor_tensor(T.hs[:], T.hp[:, 0:HW], T.zs[:], AluOpType.max).then_inc(S.act, 1)
-        g.wait_ge(S.act, 1)
-        for call in calls[rank]:
-            sent += _emit(g, T, topo, call)
+        for i, (rs, s0, ns, cl) in enumerate(stages[rank]):
+            bank = T["hp%d" % i]
+            for c, s, k in rs:
+                g.tensor.matmul(bank[:, s * TK:(s + k) * TK], T.ws[:], T.xs[:, c * TK:(c + k) * TK],
+                                True, True).then_inc(S["mm%d" % i], 1)
+            a, b = s0 * TK, (s0 + ns) * TK
+            g.vector.wait_ge(S["mm%d" % i], len(rs))
+            g.vector.tensor_tensor(T.hs[:, a:b], bank[:, a:b], T.zs[:, a:b], AluOpType.max).then_inc(S["act%d" % i], 1)
+            g.wait_ge(S["act%d" % i], 1)
+            for call in cl:
+                sent += _emit(g, T, topo, call)
 
-    for sem, n, call in fwd.get(core, []):
-        g.wait_ge(S[sem], n)
+    for need, call in fwd.get(core, []):
+        for sem, n in need:
+            g.wait_ge(S[sem], n)
         sent += _emit(g, T, topo, call)
     if sent:
         g.wait_ge(S.sent, sent)
 
-    senders = [p for p in sorted(runs, key=lambda p: (not direct[p], p)) if (p, rank) in grp]
-    if senders:
+    if rank in got:
         g.sync.dma_start(T.ws[:], T.w[:]).then_inc(S.ldw, 16)
         g.tensor.wait_ge(S.ldw, 16)
-        for i, p in enumerate(senders):
-            slot, blocks = grp[(p, rank)]
-            a, w = slot * TK, len(blocks) * TK
-            ps = T["yp%d" % p]
-            g.tensor.wait_ge(S["arr%d" % p], arrive[(p, core)])
-            g.tensor.matmul(ps[:, 0:w], T.ws[:], T.hq[:, p * HW:p * HW + w], True, True).then_inc(S["ym%d" % p], 1)
-            g.vector.wait_ge(S["ym%d" % p], 1)
-            g.vector.tensor_copy(T.ys[:, a:a + w], ps[:, 0:w]).then_inc(S["yc%d" % p], 1)
-            dq = g.scalar if i % 2 else g.sync
-            dq.wait_ge(S["yc%d" % p], 1)
-            dq.dma_start(T.y[:, a:a + w], T.ys[:, a:a + w]).then_inc(S["st%d" % p], 16)
-        for p in senders:
-            g.wait_ge(S["st%d" % p], 16)
+        copies = 0
+        for i, (sem, n, col, ps) in enumerate(got[rank]):
+            w = sum(k for p, k in ps) * TK
+            bank = T["yp%d" % i]
+            g.tensor.wait_ge(S[sem], n)
+            g.tensor.matmul(bank[:, 0:w], T.ws[:], T.hq[:, col:col + w], True, True).then_inc(S["ym%d" % i], 1)
+            g.vector.wait_ge(S["ym%d" % i], 1)
+            o = 0
+            for p, k in ps:
+                a = grp[(p, rank)][0] * TK
+                g.vector.tensor_copy(T.ys[:, a:a + k * TK], bank[:, o:o + k * TK]).then_inc(S.yc, 1)
+                o += k * TK
+                copies += 1
+        n = fill[rank] * TK
+        g.sync.wait_ge(S.yc, copies)
+        g.sync.dma_start(T.y[:, 0:n], T.ys[:, 0:n]).then_inc(S.st, 16)
+        g.wait_ge(S.st, 16)

from concourse.bass import DstId, RemoteDMATransfer
from concourse.mybir import AluOpType

SIM_CORES = 16
NPR, NBK, TK, CAP = 3, 6, 32, 8
HW = NBK * TK
HAND = 8

SCRATCH = {
    "xs": ("sbuf", [128, HW], "bfloat16"),
    "ws": ("sbuf", [128, 128], "bfloat16"),
    "zs": ("sbuf", [128, HW], "float32"),
    "hp0": ("psum", [128, 512], "float32"),
    "hp1": ("psum", [128, 512], "float32"),
    "hs": ("sbuf", [128, HW], "bfloat16"),
    "land": ("sbuf", [128, 2 * HW], "bfloat16"),
    "hq": ("sbuf", [128, 4 * HW], "bfloat16"),
    "yp0": ("psum", [128, 512], "float32"),
    "yp1": ("psum", [128, 512], "float32"),
    "yp2": ("psum", [128, 512], "float32"),
    "ys": ("sbuf", [128, CAP * TK], "bfloat16"),
}
SEMAPHORES = ["ldx", "ldw", "zf", "mm0", "mm1", "act0", "act1", "sent",
              "rin00", "rin01", "rin10", "rin11", "arr0", "arr1", "arr2", "ym0", "ym1", "ym2", "yc", "st"]


def _runs(order, a, b):
    rs = []
    for s in range(a, b):
        if rs and rs[-1][0] + rs[-1][2] == order[s]:
            rs[-1][2] += 1
        else:
            rs.append([order[s], s, 1])
    return rs


def _plan(T, topo):
    dest = T.tables["DEST"]
    cores = T.cores
    qs = sorted({q for row in dest for q in row})
    fill = {q: 0 for q in qs}
    grp = {}
    for p in range(len(dest)):
        for c, q in enumerate(dest[p]):
            if (p, q) not in grp:
                grp[(p, q)] = [fill[q], []]
            grp[(p, q)][1].append(c)
            fill[q] += 1
    wid = {k: len(v[1]) for k, v in grp.items()}

    def engines(src, dst, most=None):
        m = topo.mask(src, dst)
        e = [b for b in range(m.bit_length()) if (m >> b) & 1]
        return e if most is None else e[::len(e) // most]

    def idle_port(p):
        return [c for c in range(SIM_CORES)
                if T.rank_of(c) is None and topo.chip(c) == topo.chip(cores[p]) and topo.die(c) == topo.die(cores[p])
                and all(topo.may_write(c, cores[q]) for q in qs)][0]

    own = [p for p in range(len(dest)) if all(topo.may_write(cores[p], cores[q]) for q in qs)]
    hp = own[0]
    hub = cores[hp]
    p1, p2 = [p for p in range(len(dest)) if p != hp]
    qa, qb, qc = qs
    stages = {}
    got = {q: [] for q in qs}
    fwd = {}

    order = [c for q in qs for c in grp[(hp, q)][1]]
    cl, at = [], 0
    for q in qs:
        e = engines(hub, cores[q])
        cl.append([("hs", at * TK, wid[(hp, q)] * TK, cores[q], "hq", 0, "arr0", e)])
        got[q].append(("arr0", len(e), 0, [(hp, wid[(hp, q)])]))
        at += wid[(hp, q)]
    stages[hp] = [(_runs(order, 0, len(order)), 0, len(order), cl)]

    at = 0
    where = {}
    for k, (p, lone, rest) in enumerate(((p2, qc, [qa, qb]), (p1, qa, [qb, qc]))):
        order = grp[(p, lone)][1] + [c for q in rest for c in grp[(p, q)][1]]
        via = idle_port(p)
        n0, n1 = wid[(p, lone)], sum(wid[(p, q)] for q in rest)
        e = engines(cores[p], via, HAND)
        e2 = engines(via, cores[lone])
        stages[p] = [(_runs(order, 0, n0), 0, n0, [[("hs", 0, n0 * TK, via, "land", 0, "rin%d0" % k, e)]])]
        fwd[via] = [([("rin%d0" % k, len(e))], [("land", 0, n0 * TK, cores[lone], "hq", 3 * HW, "arr2", e2)])]
        got[lone].append(("arr2", len(e2), 3 * HW, [(p, n0)]))
        e = engines(cores[p], hub, HAND)
        stages[p].append((_runs(order, n0, n0 + n1), n0, n1,
                          [[("hs", n0 * TK, n1 * TK, hub, "land", at * TK, "rin%d1" % k, e)]]))
        where[p] = ("rin%d1" % k, len(e))
        at += n1
    joint = []
    at = 0
    for q, ps in ((qa, [p2]), (qb, [p2, p1]), (qc, [p1])):
        joint.append((q, at, [(p, wid[(p, q)]) for p in ps]))
        at += sum(wid[(p, q)] for p in ps)
    calls = {}
    for j in joint:
        calls.setdefault(sum(k for p, k in j[2]), []).append(j)
    fwd[hub] = []
    for n in sorted(calls, key=lambda n: (len(calls[n]), n)):
        js = calls[n]
        parts = [js] if len(js) in (1, 2, 4, 8) else [[j] for j in js]
        for js in parts:
            need, call = [], []
            for i, (q, a, ps) in enumerate(js):
                e = engines(hub, cores[q])
                m = len(e) // len(js)
                e = e[i * m:(i + 1) * m]
                call.append(("land", a * TK, n * TK, cores[q], "hq", HW, "arr1", e))
                need += [where[p] for p, k in ps if where[p] not in need]
                arr = ("arr1", len(e), HW, ps)
                if fwd[hub]:
                    got[q].append(arr)
                else:
                    got[q].insert(1, arr)
            fwd[hub].append((need, call))
    return grp, stages, fwd, got, fill


def _emit(g, T, topo, call):
    trs = []
    n = 0
    for w in call:
        mask = 0
        for b in w[7]:
            mask |= 1 << b
        n += len(w[7])
        a = topo.addr(w[3])
        src, dst = T[w[0]][:, w[1]:w[1] + w[2]], T[w[4]][:, w[5]:w[5] + w[2]]
        if len(call) == 1:
            g.remote_dma(dst, src, T.sem[w[6]], T.sem.sent, a[1], a[0], mask)
            return n
        trs.append(RemoteDMATransfer(dst_ids=[DstId(rid=a[0], pnc=a[1])], dma_engine_mask=mask,
                                     remote_sem=T.sem[w[6]], srcs=[src], dsts=[dst]))
    g.remote_dma_fused(trs, local_sem=T.sem.sent)
    return n


def rank_program(g, core, T, topo):
    grp, stages, fwd, got, fill = _plan(T, topo)
    rank = T.rank_of(core)
    S = T.sem
    sent = 0

    if rank in stages:
        g.sync.dma_start(T.xs[:], T.x[:]).then_inc(S.ldx, 16)
        g.scalar.dma_start(T.ws[:], T.w[:]).then_inc(S.ldw, 16)
        g.vector.memset(T.zs[:], 0.0).then_inc(S.zf, 1)
        g.tensor.wait_ge(S.ldw, 16)
        g.tensor.wait_ge(S.ldx, 16)
        g.vector.wait_ge(S.zf, 1)
        for i, (rs, s0, ns, cl) in enumerate(stages[rank]):
            bank = T["hp%d" % i]
            for c, s, k in rs:
                g.tensor.matmul(bank[:, s * TK:(s + k) * TK], T.ws[:], T.xs[:, c * TK:(c + k) * TK],
                                True, True).then_inc(S["mm%d" % i], 1)
            a, b = s0 * TK, (s0 + ns) * TK
            g.vector.wait_ge(S["mm%d" % i], len(rs))
            g.vector.tensor_tensor(T.hs[:, a:b], bank[:, a:b], T.zs[:, a:b], AluOpType.max).then_inc(S["act%d" % i], 1)
            g.wait_ge(S["act%d" % i], 1)
            for call in cl:
                sent += _emit(g, T, topo, call)

    for need, call in fwd.get(core, []):
        for sem, n in need:
            g.wait_ge(S[sem], n)
        sent += _emit(g, T, topo, call)
    if sent:
        g.wait_ge(S.sent, sent)

    if rank in got:
        g.sync.dma_start(T.ws[:], T.w[:]).then_inc(S.ldw, 16)
        g.tensor.wait_ge(S.ldw, 16)
        copies = 0
        for i, (sem, n, col, ps) in enumerate(got[rank]):
            w = sum(k for p, k in ps) * TK
            bank = T["yp%d" % i]
            g.tensor.wait_ge(S[sem], n)
            g.tensor.matmul(bank[:, 0:w], T.ws[:], T.hq[:, col:col + w], True, True).then_inc(S["ym%d" % i], 1)
            g.vector.wait_ge(S["ym%d" % i], 1)
            o = 0
            for p, k in ps:
                a = grp[(p, rank)][0] * TK
                g.vector.tensor_copy(T.ys[:, a:a + k * TK], bank[:, o:o + k * TK]).then_inc(S.yc, 1)
                o += k * TK
                copies += 1
        n = fill[rank] * TK
        g.sync.wait_ge(S.yc, copies)
        g.sync.dma_start(T.y[:, 0:n], T.ys[:, 0:n]).then_inc(S.st, 16)
        g.wait_ge(S.st, 16)
